import numpy as np
import ml_dtypes


def mxq(x, axis, fmt="e4m3"):
    dtype, down = {"e4m3": (ml_dtypes.float8_e4m3fn, 7), "e5m2": (ml_dtypes.float8_e5m2, 14)}[fmt]
    v = np.moveaxis(np.asarray(x, np.float32).astype(ml_dtypes.bfloat16).astype(np.float64), axis, -1)
    blocks = v.reshape(v.shape[:-1] + (-1, 32))
    amax = np.abs(blocks).max(-1, keepdims=True)
    byte = np.maximum(np.where(amax > 0, np.frexp(amax)[1] - 1 + 127, 0) - down, 1)
    scale = np.exp2(byte - 127.0)
    codes = (blocks / scale).astype(np.float32).astype(dtype).astype(np.float64)
    return np.moveaxis((codes * scale).reshape(v.shape), -1, axis)


WIDE = False


def mx_kscale(k):
    if not WIDE:
        return np.ones(k)
    levels = np.array([10, -10, 5, -5, 0])
    if k % 512:
        return np.exp2(np.random.permutation(np.resize(levels, k // 32))).repeat(32)
    a = np.empty((k // 512, 16))
    for p in range(k // 512):
        a[p, :8] = np.random.permutation(np.resize(levels, 8))
        for g in range(8):
            far = levels[np.abs(levels - a[p, g]) >= 10]
            a[p, g + 8] = far[np.random.randint(len(far))]
    return np.exp2(a.ravel()).repeat(32)


def f64(x):
    return np.asarray(x).astype(np.float64)


def striped(idx):
    return np.tile(np.asarray(idx).reshape(-1, 16).T, (8, 1)).astype(np.uint16)


def unstriped(offs):
    return offs[:16].T.reshape(-1).astype(np.int64)


E2M1 = np.array([0.0, 0.5, 1.0, 1.5, 2.0, 3.0, 4.0, 6.0, -0.0, -0.5, -1.0, -1.5, -2.0, -3.0, -4.0, -6.0])


def pack_weight(w, fmt):
    k, n = w.shape
    w = f64(np.asarray(w, np.float32).astype(ml_dtypes.bfloat16)).reshape(k // 32, 32, n)
    amax = np.abs(w).max(1)
    if fmt == "e4m3":
        byte = np.frexp(amax)[1] - 1 + 127 - 7
    else:
        mant, ex = np.frexp(amax / 6.0)
        byte = np.where(mant > 0.5, ex, ex - 1) + 127
    byte = np.clip(np.where(amax > 0, byte, 1), 1, 254)
    scaled = (w * np.exp2(127.0 - byte)[:, None, :]).reshape(k, n).astype(np.float32)
    by_word = np.ascontiguousarray(scaled.reshape(k // 512, 128, 4, n).transpose(0, 1, 3, 2))
    if fmt == "e4m3":
        words = by_word.astype(ml_dtypes.float8_e4m3fn).view(np.uint8)
    else:
        c = by_word.astype(ml_dtypes.float4_e2m1fn).view(np.uint8) & 0xF
        words = (c[..., 0::2] | (c[..., 1::2] << 4)).reshape(k // 512, 128, 2 * n)
    return np.ascontiguousarray(words), np.ascontiguousarray(byte.astype(np.uint8).reshape(k // 512, 16, n))


def unpack_weight(words, scales, fmt):
    g, _, n = scales.shape
    words = np.ascontiguousarray(words).reshape(g, 128, n, -1)
    if fmt == "e4m3":
        vals = words.view(ml_dtypes.float8_e4m3fn).astype(np.float64)
    else:
        nib = np.empty((g, 128, n, 4), np.uint8)
        nib[..., 0::2] = words & 0xF
        nib[..., 1::2] = words >> 4
        vals = E2M1[nib]
    vals = vals * np.repeat(np.exp2(scales.astype(np.float64) - 127.0), 8, axis=1)[..., None]
    return vals.transpose(0, 1, 3, 2).reshape(g * 512, n)


K, T, J, S, R, G, N = 1024, 1024, 384, 512, 512, 48, 256


def setup_inputs():
    n = np.random.standard_normal
    idx = np.random.permutation(T)[:J]
    idx2 = np.random.permutation(S)[:J]
    fk = mx_kscale(K)
    fr = mx_kscale(R)
    wp = pack_weight(n((K, R)) * 1 / np.sqrt(K) * fk[:, None] * fr, "e2m1")
    wbp = pack_weight(n((R, N)) * 1 / np.sqrt(R) / fr[:, None], "e2m1")
    return {
        "xa": (n((K, T))).astype(np.float32),
        "xb": (n((K, S))).astype(np.float32),
        "fk": (np.random.uniform(0.5, 2.0, (K, 1)) / fk[:, None]).astype(np.float32),
        "w_words": wp[0],
        "w_scales": wp[1],
        "wb_words": wbp[0],
        "wb_scales": wbp[1],
        "rs": (1.0 * n((J, N))).astype(np.float32),
        "offs": striped(idx),
        "offs2": striped(idx2),
    }


def reference(xa, xb, fk, w_words, w_scales, wb_words, wb_scales, rs, offs, offs2):
    idx = unstriped(offs)
    idx2 = unstriped(offs2)
    wu = unpack_weight(w_words, w_scales, "e2m1")
    wbu = unpack_weight(wb_words, wb_scales, "e2m1")
    u = f64(xa)[:, idx] * f64(xb)[:, idx2] * f64(fk)
    uq = mxq(u, 0, "e4m3")
    a = wu.T @ uq
    m1 = a.reshape(R, G, J // G).mean(axis=2)
    m2 = np.repeat(m1, J // G, axis=1)
    hid = a - m2
    hidq = mxq(hid, 0, "e4m3")
    p = hidq.T @ wbu
    mn = np.mean(np.abs(p), axis=1, keepdims=True)
    y = np.maximum(p - mn, 0.0) - 0.3 * f64(rs)
    return y

@@ -1,0 +1,216 @@
+from contextlib import ExitStack
+
+import concourse.mybir as mybir
+
+K, T, J, S, R, N = 1024, 1024, 384, 512, 512, 256
+FLOPS = 2 * K * R * J + 2 * R * J * N
+
+F32 = mybir.dt.float32
+BF16 = mybir.dt.bfloat16
+I32 = mybir.dt.int32
+U32 = mybir.dt.uint32
+U16 = mybir.dt.uint16
+U8 = mybir.dt.uint8
+FP8X4 = mybir.dt.float8_e4m3fn_x4
+FP4X4 = mybir.dt.float4_e2m1fn_x4
+ALU = mybir.AluOpType
+ACT = mybir.ActivationFunctionType
+AXIS = mybir.AxisListType
+
+P = 128
+PACK = 4
+K_PASS = P * PACK
+PASSES = K // K_PASS
+CHUNK = 128
+CHUNKS = J // CHUNK
+BUNDLE = 8
+LIST_COLS = CHUNK // 16
+QUADRANTS = 4
+
+
+def tile_list_entryproducts_levelled_rowabove_kernel(
+    tc, xa, xb, fk, w_words, w_scales, wb_words, wb_scales, rs, offs, offs2, out
+):
+    nc = tc.nc
+    with ExitStack() as ctx:
+        keep = ctx.enter_context(tc.tile_pool(name="keep", bufs=1))
+        psum = ctx.enter_context(tc.psum_pool(name="psum", bufs=1))
+
+        list_a = keep.tile([P, J // 16], U16, name="list_a")
+        list_b = keep.tile([P, J // 16], U16, name="list_b")
+        factor = keep.tile([P, PASSES, PACK], F32, name="factor")
+        w_raw = keep.tile([P, PASSES, R], U16, name="w_raw", align_bytes=64)
+        w_scale_raw = keep.tile([P, PASSES, R], U8, name="w_scale_raw", align_bytes=64)
+        w_codes = keep.tile([P, PASSES, R], U16, name="w_codes", align_bytes=64)
+        w_scale = keep.tile([P, PASSES, R], U8, name="w_scale", align_bytes=64)
+        wb_codes = keep.tile([P, 2 * N], U8, name="wb_codes", align_bytes=64)
+        wb_scale = keep.tile([P, N], U8, name="wb_scale", align_bytes=64)
+        residual = keep.tile([P, CHUNKS, N], F32, name="residual")
+        xa_plane = [[keep.tile([P, T], F32, name="xa_%d_%d" % (z, t)) for t in range(PACK)] for z in range(PASSES)]
+        xb_pair = [[keep.tile([P, 2 * S], F32, name="xb_%d_%d" % (z, h)) for h in range(2)] for z in range(PASSES)]
+
+        nc.vector.memset(w_scale_raw[:].bitcast(I32), 0)
+        nc.vector.memset(wb_scale[:].bitcast(I32), 0)
+
+        def load_w_scales():
+            for q in range(QUADRANTS):
+                nc.sync.dma_start(
+                    out=w_scale_raw[32 * q : 32 * q + 4, :, :].bitcast(I32),
+                    in_=w_scales[:, 4 * q : 4 * q + 4, :].rearrange("z r c -> r z c").bitcast(I32),
+                )
+
+        def load_wb_scales():
+            for q in range(QUADRANTS):
+                nc.sync.dma_start(
+                    out=wb_scale[32 * q : 32 * q + 4, :].bitcast(I32),
+                    in_=wb_scales[0, 4 * q : 4 * q + 4, :].bitcast(I32),
+                )
+
+        def load_xb(z, h):
+            rows = xb[z * K_PASS : (z + 1) * K_PASS, :].rearrange("(p t) s -> p (t s)", t=PACK)
+            nc.sync.dma_start(out=xb_pair[z][h][:], in_=rows[:, 2 * h * S : (2 * h + 2) * S])
+
+        def load_xa(z, t):
+            rows = xa[z * K_PASS : (z + 1) * K_PASS, :].rearrange("(p t) c -> p (t c)", t=PACK)
+            nc.sync.dma_start(out=xa_plane[z][t][:], in_=rows[:, t * T : (t + 1) * T])
+
+        nc.sync.dma_start(list_b[:], offs2)
+        nc.sync.dma_start(list_a[:], offs)
+        nc.sync.dma_start(out=w_raw[:].bitcast(I32), in_=w_words.rearrange("z p b -> p z b").bitcast(I32))
+        for z in range(PASSES):
+            for h in range(2):
+                load_xb(z, h)
+                if z == 0 and h == 0:
+                    nc.sync.dma_start(out=factor[:], in_=fk.rearrange("(z p t) o -> p z (t o)", z=PASSES, t=PACK))
+                load_xa(z, 2 * h)
+                load_xa(z, 2 * h + 1)
+                if z == 0 and h == 0:
+                    load_w_scales()
+                if z == 0 and h == 1:
+                    load_wb_scales()
+        nc.sync.dma_start(out=wb_codes[:].bitcast(I32), in_=wb_words[0].bitcast(I32))
+        nc.sync.dma_start(out=residual[:], in_=rs.rearrange("(c p) n -> p c n", p=P))
+
+        nc.vector.tensor_copy(
+            out=w_codes[:].rearrange("p z (t c i) -> p z c t i", t=PACK, i=8),
+            in_=w_raw[:].rearrange("p z (c i t) -> p z c t i", t=PACK, i=8),
+        )
+
+        a_bank = [psum.tile([P, PACK, CHUNK], F32, name="a_%d" % c) for c in range(CHUNKS)]
+        p_bank = [psum.tile([P, N], F32, name="p_%d" % c) for c in range(CHUNKS)]
+
+        def interleave(engine_copy, grouped, planes):
+            engine_copy(
+                out=grouped.rearrange("p (c i t) -> p c t i", t=PACK, i=4),
+                in_=planes.rearrange("p t (c i) -> p c t i", i=4),
+            )
+
+        def first_matmuls(z, c, codes, scales):
+            for t in range(PACK):
+                cols = slice(t * P, (t + 1) * P)
+                nc.tensor.matmul_mx(
+                    out=a_bank[c][:, t, :],
+                    lhsT=w_codes[:, z, cols].bitcast(FP4X4),
+                    lhsT_scale=w_scale[:, z, cols],
+                    rhs=codes.bitcast(FP8X4),
+                    rhs_scale=scales,
+                    start=(z == 0 and t == 0),
+                    stop=(z == PASSES - 1 and t == PACK - 1),
+                )
+
+        for z in range(PASSES):
+            u_planes = keep.tile([P, CHUNKS, PACK, CHUNK], BF16, name="u_planes_%d" % z)
+            u_grouped = [keep.tile([P, CHUNK * PACK], BF16, name="u_grouped_%d_%d" % (z, c), align_bytes=64) for c in range(CHUNKS)]
+            u_codes = [keep.tile([P, CHUNK], U32, name="u_codes_%d_%d" % (z, c), align_bytes=64) for c in range(CHUNKS)]
+            u_scale = [keep.tile([P, CHUNK], U8, name="u_scale_%d_%d" % (z, c), align_bytes=64) for c in range(CHUNKS)]
+            for t in range(PACK):
+                h, odd = divmod(t, 2)
+                picked_b = keep.tile([P, J], F32, name="picked_b_%d_%d" % (z, t))
+                if odd:
+                    nc.vector.tensor_copy(out=picked_b[:], in_=xb_pair[z][h][:, S : 2 * S].indirect(list_b[:]))
+                else:
+                    nc.scalar.activation(picked_b[:], xb_pair[z][h][:].indirect(list_b[:]), ACT.Copy)
+                if z == PASSES - 1 and t == PACK - 1:
+                    for c in range(CHUNKS):
+                        picked_a = keep.tile([P, CHUNK], F32, name="picked_a_last_%d" % c)
+                        window = xa_plane[z][t][:].indirect(list_a[:, c * LIST_COLS : (c + 1) * LIST_COLS])
+                        if c == 0:
+                            nc.vector.tensor_copy(out=picked_a[:], in_=window)
+                        else:
+                            nc.scalar.activation(picked_a[:], window, ACT.Copy)
+                        nc.vector.scalar_tensor_tensor(
+                            out=u_planes[:, c, t, :],
+                            in0=picked_a[:],
+                            scalar=factor[:, z, t : t + 1],
+                            in1=picked_b[:, c * CHUNK : (c + 1) * CHUNK],
+                            op0=ALU.mult,
+                            op1=ALU.mult,
+                        )
+                else:
+                    picked_a = keep.tile([P, J], F32, name="picked_a_%d_%d" % (z, t))
+                    nc.scalar.activation(picked_a[:], xa_plane[z][t][:].indirect(list_a[:]), ACT.Copy)
+                    nc.vector.scalar_tensor_tensor(
+                        out=u_planes[:, :, t, :],
+                        in0=picked_a[:].rearrange("p (c j) -> p c j", c=CHUNKS),
+                        scalar=factor[:, z, t : t + 1],
+                        in1=picked_b[:].rearrange("p (c j) -> p c j", c=CHUNKS),
+                        op0=ALU.mult,
+                        op1=ALU.mult,
+                    )
+            if z == 0:
+                nc.vector.tensor_copy(
+                    out=w_scale[:].rearrange("p z (t c i) -> p z c t i", t=PACK, i=16),
+                    in_=w_scale_raw[:].rearrange("p z (c i t) -> p z c t i", t=PACK, i=16),
+                )
+            for c in range(CHUNKS):
+                on_scalar = z == PASSES - 1 and c > 0
+                interleave(nc.scalar.copy if on_scalar else nc.vector.tensor_copy, u_grouped[c][:], u_planes[:, c, :, :])
+            for c in range(CHUNKS):
+                nc.vector.quantize_mx(out=u_codes[c][:].bitcast(FP8X4), scales=u_scale[c][:], in_=u_grouped[c][:])
+                first_matmuls(z, c, u_codes[c][:], u_scale[c][:])
+
+        groups = CHUNK // BUNDLE
+        for c in range(CHUNKS):
+            sums = keep.tile([P, groups, PACK], F32, name="sums_%d" % c)
+            means = keep.tile([P, groups, PACK], F32, name="means_%d" % c)
+            hid = keep.tile([P, CHUNK * PACK], BF16, name="hid_%d" % c, align_bytes=64)
+            hid_codes = keep.tile([P, CHUNK], U32, name="hid_codes_%d" % c, align_bytes=64)
+            hid_scale = keep.tile([P, CHUNK], U8, name="hid_scale_%d" % c, align_bytes=64)
+            nc.vector.tensor_reduce(
+                out=sums[:], in_=a_bank[c][:].rearrange("p t (g i) -> p g t i", i=BUNDLE), axis=AXIS.X, op=ALU.add
+            )
+            nc.vector.tensor_scalar(out=means[:], in0=sums[:], scalar1=1.0 / BUNDLE, scalar2=None, op0=ALU.mult)
+            nc.vector.tensor_tensor(
+                out=hid[:].rearrange("p (g i t) -> p g i t", i=BUNDLE, t=PACK),
+                in0=a_bank[c][:].rearrange("p t (g i) -> p g i t", i=BUNDLE),
+                in1=means[:].unsqueeze(2).to_broadcast([P, groups, BUNDLE, PACK]),
+                op=ALU.subtract,
+            )
+            nc.vector.quantize_mx(out=hid_codes[:].bitcast(FP8X4), scales=hid_scale[:], in_=hid[:])
+            nc.tensor.matmul_mx(
+                out=p_bank[c][:],
+                lhsT=hid_codes[:].bitcast(FP8X4),
+                lhsT_scale=hid_scale[:],
+                rhs=wb_codes[:].bitcast(FP4X4),
+                rhs_scale=wb_scale[:],
+                start=True,
+                stop=True,
+            )
+        for c in range(CHUNKS):
+            magnitude = keep.tile([P, N], F32, name="magnitude_%d" % c)
+            level = keep.tile([P, 1], F32, name="level_%d" % c)
+            above = keep.tile([P, N], F32, name="above_%d" % c)
+            result = keep.tile([P, N], F32, name="result_%d" % c)
+            nc.scalar.activation(magnitude[:], p_bank[c][:], ACT.Abs, scale=1.0 / N, accum_out=level[:])
+            if c == CHUNKS - 1:
+                nc.vector.tensor_scalar(
+                    out=above[:], in0=p_bank[c][:], scalar1=level[:], scalar2=0.0, op0=ALU.subtract, op1=ALU.max
+                )
+            else:
+                minus_level = keep.tile([P, 1], F32, name="minus_level_%d" % c)
+                nc.scalar.activation(minus_level[:], level[:], ACT.Copy, scale=-1.0)
+                nc.scalar.activation(above[:], p_bank[c][:], ACT.Relu, bias=minus_level[:])
+            nc.vector.scalar_tensor_tensor(
+                out=result[:], in0=residual[:, c, :], scalar=-0.3, in1=above[:], op0=ALU.mult, op1=ALU.add
+            )
+            nc.sync.dma_start(out=out[c * CHUNK : (c + 1) * CHUNK, :], in_=result[:])

@@ -74,26 +74,33 @@ def tile_list_entryproducts_levelled_rowabove_kernel(
             rows = xa[z * K_PASS : (z + 1) * K_PASS, :].rearrange("(p t) c -> p (t c)", t=PACK)
             nc.sync.dma_start(out=xa_plane[z][t][:], in_=rows[:, t * T : (t + 1) * T])
 
+        load_xb(0, 0)
         nc.sync.dma_start(list_b[:], offs2)
+        load_xa(0, 0)
         nc.sync.dma_start(list_a[:], offs)
+        nc.sync.dma_start(out=factor[:], in_=fk.rearrange("(z p t) o -> p z (t o)", z=PASSES, t=PACK))
         nc.sync.dma_start(out=w_raw[:].bitcast(I32), in_=w_words.rearrange("z p b -> p z b").bitcast(I32))
-        for z in range(PASSES):
-            for h in range(2):
-                load_xb(z, h)
-                if z == 0 and h == 0:
-                    nc.sync.dma_start(out=factor[:], in_=fk.rearrange("(z p t) o -> p z (t o)", z=PASSES, t=PACK))
-                load_xa(z, 2 * h)
-                load_xa(z, 2 * h + 1)
-                if z == 0 and h == 0:
-                    load_w_scales()
-                if z == 0 and h == 1:
-                    load_wb_scales()
+        load_xa(0, 1)
+        load_xb(0, 1)
+        load_w_scales()
+        load_xa(0, 2)
+        load_xa(0, 3)
+        for h in range(2):
+            load_xb(1, h)
+        for t in range(PACK):
+            load_xa(1, t)
         nc.sync.dma_start(out=wb_codes[:].bitcast(I32), in_=wb_words[0].bitcast(I32))
+        load_wb_scales()
         nc.sync.dma_start(out=residual[:], in_=rs.rearrange("(c p) n -> p c n", p=P))
 
         nc.vector.tensor_copy(
             out=w_codes[:].rearrange("p z (t c i) -> p z c t i", t=PACK, i=8),
             in_=w_raw[:].rearrange("p z (c i t) -> p z c t i", t=PACK, i=8),
+        )
+
+        nc.vector.tensor_copy(
+            out=w_scale[:].rearrange("p z (t c i) -> p z c t i", t=PACK, i=16),
+            in_=w_scale_raw[:].rearrange("p z (c i t) -> p z c t i", t=PACK, i=16),
         )
 
         a_bank = [psum.tile([P, PACK, CHUNK], F32, name="a_%d" % c) for c in range(CHUNKS)]
@@ -118,56 +125,60 @@ def tile_list_entryproducts_levelled_rowabove_kernel(
                     stop=(z == PASSES - 1 and t == PACK - 1),
                 )
 
-        for z in range(PASSES):
-            u_planes = keep.tile([P, CHUNKS, PACK, CHUNK], BF16, name="u_planes_%d" % z)
-            u_grouped = [keep.tile([P, CHUNK * PACK], BF16, name="u_grouped_%d_%d" % (z, c), align_bytes=64) for c in range(CHUNKS)]
-            u_codes = [keep.tile([P, CHUNK], U32, name="u_codes_%d_%d" % (z, c), align_bytes=64) for c in range(CHUNKS)]
-            u_scale = [keep.tile([P, CHUNK], U8, name="u_scale_%d_%d" % (z, c), align_bytes=64) for c in range(CHUNKS)]
-            for t in range(PACK):
-                h, odd = divmod(t, 2)
-                picked_b = keep.tile([P, J], F32, name="picked_b_%d_%d" % (z, t))
-                if odd:
-                    nc.vector.tensor_copy(out=picked_b[:], in_=xb_pair[z][h][:, S : 2 * S].indirect(list_b[:]))
-                else:
-                    nc.scalar.activation(picked_b[:], xb_pair[z][h][:].indirect(list_b[:]), ACT.Copy)
-                if z == PASSES - 1 and t == PACK - 1:
-                    for c in range(CHUNKS):
-                        picked_a = keep.tile([P, CHUNK], F32, name="picked_a_last_%d" % c)
-                        window = xa_plane[z][t][:].indirect(list_a[:, c * LIST_COLS : (c + 1) * LIST_COLS])
-                        if c == 0:
-                            nc.vector.tensor_copy(out=picked_a[:], in_=window)
-                        else:
-                            nc.scalar.activation(picked_a[:], window, ACT.Copy)
-                        nc.vector.scalar_tensor_tensor(
-                            out=u_planes[:, c, t, :],
-                            in0=picked_a[:],
-                            scalar=factor[:, z, t : t + 1],
-                            in1=picked_b[:, c * CHUNK : (c + 1) * CHUNK],
-                            op0=ALU.mult,
-                            op1=ALU.mult,
-                        )
-                else:
-                    picked_a = keep.tile([P, J], F32, name="picked_a_%d_%d" % (z, t))
-                    nc.scalar.activation(picked_a[:], xa_plane[z][t][:].indirect(list_a[:]), ACT.Copy)
-                    nc.vector.scalar_tensor_tensor(
-                        out=u_planes[:, :, t, :],
-                        in0=picked_a[:].rearrange("p (c j) -> p c j", c=CHUNKS),
-                        scalar=factor[:, z, t : t + 1],
-                        in1=picked_b[:].rearrange("p (c j) -> p c j", c=CHUNKS),
-                        op0=ALU.mult,
-                        op1=ALU.mult,
-                    )
-            if z == 0:
-                nc.vector.tensor_copy(
-                    out=w_scale[:].rearrange("p z (t c i) -> p z c t i", t=PACK, i=16),
-                    in_=w_scale_raw[:].rearrange("p z (c i t) -> p z c t i", t=PACK, i=16),
+        spans = [[(0, J)], [(c * CHUNK, CHUNK) for c in range(CHUNKS)]]
+        u_planes = [
+            [keep.tile([P, PACK, width], F32, name="u_planes_%d_%d" % (z, first)) for first, width in spans[z]]
+            for z in range(PASSES)
+        ]
+
+        def pick_b(z, t):
+            h, odd = divmod(t, 2)
+            picked_b = keep.tile([P, J], F32, name="picked_b_%d_%d" % (z, t))
+            if odd:
+                nc.vector.tensor_copy(out=picked_b[:], in_=xb_pair[z][h][:, S : 2 * S].indirect(list_b[:]))
+            else:
+                nc.scalar.activation(picked_b[:], xb_pair[z][h][:].indirect(list_b[:]), ACT.Copy)
+            return picked_b
+
+        def product(z, t, s, picked_b):
+            first, width = spans[z][s]
+            listed = xa_plane[z][t][:].indirect(list_a[:, first // 16 : (first + width) // 16])
+            b_cols = picked_b[:, first : first + width]
+            if (z, t, s) == (PASSES - 1, PACK - 1, 0):
+                scaled_b = keep.tile([P, width], F32, name="scaled_b")
+                nc.vector.tensor_scalar(
+                    out=scaled_b[:], in0=b_cols, scalar1=factor[:, z, t : t + 1], scalar2=None, op0=ALU.mult
                 )
-            for c in range(CHUNKS):
-                on_scalar = z == PASSES - 1 and c > 0
-                interleave(nc.scalar.copy if on_scalar else nc.vector.tensor_copy, u_grouped[c][:], u_planes[:, c, :, :])
-            for c in range(CHUNKS):
-                nc.vector.quantize_mx(out=u_codes[c][:].bitcast(FP8X4), scales=u_scale[c][:], in_=u_grouped[c][:])
-                first_matmuls(z, c, u_codes[c][:], u_scale[c][:])
+                nc.vector.tensor_tensor(out=u_planes[z][s][:, t, :], in0=listed, in1=scaled_b[:], op=ALU.mult)
+            else:
+                picked_a = keep.tile([P, width], F32, name="picked_a_%d_%d_%d" % (z, t, s))
+                nc.scalar.activation(picked_a[:], listed, ACT.Copy)
+                nc.vector.scalar_tensor_tensor(
+                    out=u_planes[z][s][:, t, :],
+                    in0=picked_a[:],
+                    scalar=factor[:, z, t : t + 1],
+                    in1=b_cols,
+                    op0=ALU.mult,
+                    op1=ALU.mult,
+                )
+
+        def quantise_and_multiply(z, s, engine_copy):
+            first, width = spans[z][s]
+            grouped = keep.tile([P, width * PACK], BF16, name="u_grouped_%d_%d" % (z, s), align_bytes=64)
+            codes = keep.tile([P, width], U32, name="u_codes_%d_%d" % (z, s), align_bytes=64)
+            scales = keep.tile([P, width], U8, name="u_scale_%d_%d" % (z, s), align_bytes=64)
+            interleave(engine_copy, grouped[:], u_planes[z][s][:])
+            nc.vector.quantize_mx(out=codes[:].bitcast(FP8X4), scales=scales[:], in_=grouped[:])
+            for col in range(0, width, CHUNK):
+                first_matmuls(z, (first + col) // CHUNK, codes[:, col : col + CHUNK], scales[:, col : col + CHUNK])
+
+        for z in range(PASSES):
+            for t in range(PACK):
+                picked_b = pick_b(z, t)
+                for s in range(len(spans[z])):
+                    product(z, t, s, picked_b)
+                    if t == PACK - 1:
+                        quantise_and_multiply(z, s, nc.scalar.copy if s > 0 else nc.vector.tensor_copy)
 
         groups = CHUNK // BUNDLE
         for c in range(CHUNKS):
@@ -179,7 +190,7 @@ def tile_list_entryproducts_levelled_rowabove_kernel(
             nc.vector.tensor_reduce(
                 out=sums[:], in_=a_bank[c][:].rearrange("p t (g i) -> p g t i", i=BUNDLE), axis=AXIS.X, op=ALU.add
             )
-            nc.vector.tensor_scalar(out=means[:], in0=sums[:], scalar1=1.0 / BUNDLE, scalar2=None, op0=ALU.mult)
+            nc.scalar.activation(means[:], sums[:], ACT.Copy, scale=1.0 / BUNDLE)
             nc.vector.tensor_tensor(
                 out=hid[:].rearrange("p (g i t) -> p g i t", i=BUNDLE, t=PACK),
                 in0=a_bank[c][:].rearrange("p t (g i) -> p g i t", i=BUNDLE),

@@ -26,6 +26,7 @@ CHUNKS = J // CHUNK
 BUNDLE = 8
 LIST_COLS = CHUNK // 16
 QUADRANTS = 4
+LATE_PLANES = 2
 
 
 def tile_list_entryproducts_levelled_rowabove_kernel(
@@ -79,10 +80,10 @@ def tile_list_entryproducts_levelled_rowabove_kernel(
         load_xa(0, 0)
         nc.sync.dma_start(list_a[:], offs)
         nc.sync.dma_start(out=factor[:], in_=fk.rearrange("(z p t) o -> p z (t o)", z=PASSES, t=PACK))
-        nc.sync.dma_start(out=w_raw[:].bitcast(I32), in_=w_words.rearrange("z p b -> p z b").bitcast(I32))
         load_xa(0, 1)
-        load_xb(0, 1)
+        nc.sync.dma_start(out=w_raw[:].bitcast(I32), in_=w_words.rearrange("z p b -> p z b").bitcast(I32))
         load_w_scales()
+        load_xb(0, 1)
         load_xa(0, 2)
         load_xa(0, 3)
         for h in range(2):
@@ -140,27 +141,30 @@ def tile_list_entryproducts_levelled_rowabove_kernel(
                 nc.scalar.activation(picked_b[:], xb_pair[z][h][:].indirect(list_b[:]), ACT.Copy)
             return picked_b
 
-        def product(z, t, s, picked_b):
-            first, width = spans[z][s]
+        def pick_a(z, t, first, width):
+            picked_a = keep.tile([P, width], F32, name="picked_a_%d_%d_%d" % (z, t, first))
             listed = xa_plane[z][t][:].indirect(list_a[:, first // 16 : (first + width) // 16])
-            b_cols = picked_b[:, first : first + width]
-            if (z, t, s) == (PASSES - 1, PACK - 1, 0):
-                scaled_b = keep.tile([P, width], F32, name="scaled_b")
-                nc.vector.tensor_scalar(
-                    out=scaled_b[:], in0=b_cols, scalar1=factor[:, z, t : t + 1], scalar2=None, op0=ALU.mult
-                )
-                nc.vector.tensor_tensor(out=u_planes[z][s][:, t, :], in0=listed, in1=scaled_b[:], op=ALU.mult)
-            else:
-                picked_a = keep.tile([P, width], F32, name="picked_a_%d_%d_%d" % (z, t, s))
-                nc.scalar.activation(picked_a[:], listed, ACT.Copy)
-                nc.vector.scalar_tensor_tensor(
-                    out=u_planes[z][s][:, t, :],
-                    in0=picked_a[:],
-                    scalar=factor[:, z, t : t + 1],
-                    in1=b_cols,
-                    op0=ALU.mult,
-                    op1=ALU.mult,
-                )
+            nc.scalar.activation(picked_a[:], listed, ACT.Copy)
+            return picked_a
+
+        def product(z, t, s, a_cols, picked_b):
+            first, width = spans[z][s]
+            nc.vector.scalar_tensor_tensor(
+                out=u_planes[z][s][:, t, :],
+                in0=a_cols,
+                scalar=factor[:, z, t : t + 1],
+                in1=picked_b[:, first : first + width],
+                op0=ALU.mult,
+                op1=ALU.mult,
+            )
+
+        def fused_product(z, t, picked_b):
+            scaled_b = keep.tile([P, CHUNK], F32, name="scaled_b_%d" % t)
+            nc.vector.tensor_scalar(
+                out=scaled_b[:], in0=picked_b[:, :CHUNK], scalar1=factor[:, z, t : t + 1], scalar2=None, op0=ALU.mult
+            )
+            listed = xa_plane[z][t][:].indirect(list_a[:, :LIST_COLS])
+            nc.vector.tensor_tensor(out=u_planes[z][0][:, t, :], in0=listed, in1=scaled_b[:], op=ALU.mult)
 
         def quantise_and_multiply(z, s, engine_copy):
             first, width = spans[z][s]
@@ -175,29 +179,44 @@ def tile_list_entryproducts_levelled_rowabove_kernel(
         for z in range(PASSES):
             for t in range(PACK):
                 picked_b = pick_b(z, t)
-                for s in range(len(spans[z])):
-                    product(z, t, s, picked_b)
+                late = z == PASSES - 1 and t >= PACK - LATE_PLANES
+                if not late:
+                    picked_a = pick_a(z, t, 0, J)
+                for s, (first, width) in enumerate(spans[z]):
+                    if not late:
+                        product(z, t, s, picked_a[:, first : first + width], picked_b)
+                    elif s == 0:
+                        fused_product(z, t, picked_b)
+                    else:
+                        product(z, t, s, pick_a(z, t, first, width)[:], picked_b)
                     if t == PACK - 1:
                         quantise_and_multiply(z, s, nc.scalar.copy if s > 0 else nc.vector.tensor_copy)
 
         groups = CHUNK // BUNDLE
-        for c in range(CHUNKS):
+        means = [keep.tile([P, groups, PACK], F32, name="means_%d" % c) for c in range(CHUNKS)]
+        hid = [keep.tile([P, CHUNK * PACK], BF16, name="hid_%d" % c, align_bytes=64) for c in range(CHUNKS)]
+        level = [keep.tile([P, 1], F32, name="level_%d" % c) for c in range(CHUNKS)]
+
+        def bundle_means(c):
             sums = keep.tile([P, groups, PACK], F32, name="sums_%d" % c)
-            means = keep.tile([P, groups, PACK], F32, name="means_%d" % c)
-            hid = keep.tile([P, CHUNK * PACK], BF16, name="hid_%d" % c, align_bytes=64)
-            hid_codes = keep.tile([P, CHUNK], U32, name="hid_codes_%d" % c, align_bytes=64)
-            hid_scale = keep.tile([P, CHUNK], U8, name="hid_scale_%d" % c, align_bytes=64)
             nc.vector.tensor_reduce(
                 out=sums[:], in_=a_bank[c][:].rearrange("p t (g i) -> p g t i", i=BUNDLE), axis=AXIS.X, op=ALU.add
             )
-            nc.scalar.activation(means[:], sums[:], ACT.Copy, scale=1.0 / BUNDLE)
+            nc.scalar.activation(means[c][:], sums[:], ACT.Copy, scale=1.0 / BUNDLE)
+
+        def take_means_off(c):
             nc.vector.tensor_tensor(
-                out=hid[:].rearrange("p (g i t) -> p g i t", i=BUNDLE, t=PACK),
+                out=hid[c][:].rearrange("p (g i t) -> p g i t", i=BUNDLE, t=PACK),
                 in0=a_bank[c][:].rearrange("p t (g i) -> p g i t", i=BUNDLE),
-                in1=means[:].unsqueeze(2).to_broadcast([P, groups, BUNDLE, PACK]),
+                in1=means[c][:].unsqueeze(2).to_broadcast([P, groups, BUNDLE, PACK]),
                 op=ALU.subtract,
             )
-            nc.vector.quantize_mx(out=hid_codes[:].bitcast(FP8X4), scales=hid_scale[:], in_=hid[:])
+
+        def second_product(c):
+            hid_codes = keep.tile([P, CHUNK], U32, name="hid_codes_%d" % c, align_bytes=64)
+            hid_scale = keep.tile([P, CHUNK], U8, name="hid_scale_%d" % c, align_bytes=64)
+            magnitude = keep.tile([P, N], F32, name="magnitude_%d" % c)
+            nc.vector.quantize_mx(out=hid_codes[:].bitcast(FP8X4), scales=hid_scale[:], in_=hid[c][:])
             nc.tensor.matmul_mx(
                 out=p_bank[c][:],
                 lhsT=hid_codes[:].bitcast(FP8X4),
@@ -207,21 +226,32 @@ def tile_list_entryproducts_levelled_rowabove_kernel(
                 start=True,
                 stop=True,
             )
-        for c in range(CHUNKS):
-            magnitude = keep.tile([P, N], F32, name="magnitude_%d" % c)
-            level = keep.tile([P, 1], F32, name="level_%d" % c)
+            nc.scalar.activation(magnitude[:], p_bank[c][:], ACT.Abs, scale=1.0 / N, accum_out=level[c][:])
+
+        def finish(c):
             above = keep.tile([P, N], F32, name="above_%d" % c)
             result = keep.tile([P, N], F32, name="result_%d" % c)
-            nc.scalar.activation(magnitude[:], p_bank[c][:], ACT.Abs, scale=1.0 / N, accum_out=level[:])
-            if c == CHUNKS - 1:
-                nc.vector.tensor_scalar(
-                    out=above[:], in0=p_bank[c][:], scalar1=level[:], scalar2=0.0, op0=ALU.subtract, op1=ALU.max
-                )
-            else:
-                minus_level = keep.tile([P, 1], F32, name="minus_level_%d" % c)
-                nc.scalar.activation(minus_level[:], level[:], ACT.Copy, scale=-1.0)
+            if c == 0:
+                minus_level = keep.tile([P, 1], F32, name="minus_level")
+                nc.scalar.activation(minus_level[:], level[c][:], ACT.Copy, scale=-1.0)
                 nc.scalar.activation(above[:], p_bank[c][:], ACT.Relu, bias=minus_level[:])
+            else:
+                nc.vector.tensor_scalar(
+                    out=above[:], in0=p_bank[c][:], scalar1=level[c][:], scalar2=0.0, op0=ALU.subtract, op1=ALU.max
+                )
             nc.vector.scalar_tensor_tensor(
                 out=result[:], in0=residual[:, c, :], scalar=-0.3, in1=above[:], op0=ALU.mult, op1=ALU.add
             )
             nc.sync.dma_start(out=out[c * CHUNK : (c + 1) * CHUNK, :], in_=result[:])
+
+        bundle_means(0)
+        bundle_means(1)
+        take_means_off(0)
+        take_means_off(1)
+        bundle_means(2)
+        second_product(0)
+        second_product(1)
+        take_means_off(2)
+        second_product(2)
+        for c in range(CHUNKS):
+            finish(c)

@@ -53,6 +53,11 @@ def tile_list_entryproducts_levelled_rowabove_kernel(
         nc.vector.memset(w_scale_raw[:].bitcast(I32), 0)
         nc.vector.memset(wb_scale[:].bitcast(I32), 0)
 
+        warm_in = keep.tile([P, 1], F32, name="warm_in")
+        warm_out = keep.tile([P, 1], F32, name="warm_out")
+        nc.vector.memset(warm_in[:], 0.0)
+        nc.scalar.activation(warm_out[:], warm_in[:], ACT.Copy)
+
         def load_w_scales():
             for q in range(QUADRANTS):
                 nc.sync.dma_start(

from contextlib import ExitStack

import concourse.mybir as mybir

K, T, J, S, R, N = 1024, 1024, 384, 512, 512, 256
FLOPS = 2 * K * R * J + 2 * R * J * N

F32 = mybir.dt.float32
BF16 = mybir.dt.bfloat16
I32 = mybir.dt.int32
U32 = mybir.dt.uint32
U16 = mybir.dt.uint16
U8 = mybir.dt.uint8
FP8X4 = mybir.dt.float8_e4m3fn_x4
FP4X4 = mybir.dt.float4_e2m1fn_x4
ALU = mybir.AluOpType
ACT = mybir.ActivationFunctionType
AXIS = mybir.AxisListType

P = 128
PACK = 4
K_PASS = P * PACK
PASSES = K // K_PASS
CHUNK = 128
CHUNKS = J // CHUNK
BUNDLE = 8
LIST_COLS = CHUNK // 16
QUADRANTS = 4
LATE_PLANES = 2


def tile_list_entryproducts_levelled_rowabove_kernel(
    tc, xa, xb, fk, w_words, w_scales, wb_words, wb_scales, rs, offs, offs2, out
):
    nc = tc.nc
    with ExitStack() as ctx:
        keep = ctx.enter_context(tc.tile_pool(name="keep", bufs=1))
        psum = ctx.enter_context(tc.psum_pool(name="psum", bufs=1))

        list_a = keep.tile([P, J // 16], U16, name="list_a")
        list_b = keep.tile([P, J // 16], U16, name="list_b")
        factor = keep.tile([P, PASSES, PACK], F32, name="factor")
        w_raw = keep.tile([P, PASSES, R], U16, name="w_raw", align_bytes=64)
        w_scale_raw = keep.tile([P, PASSES, R], U8, name="w_scale_raw", align_bytes=64)
        w_codes = keep.tile([P, PASSES, R], U16, name="w_codes", align_bytes=64)
        w_scale = keep.tile([P, PASSES, R], U8, name="w_scale", align_bytes=64)
        wb_codes = keep.tile([P, 2 * N], U8, name="wb_codes", align_bytes=64)
        wb_scale = keep.tile([P, N], U8, name="wb_scale", align_bytes=64)
        residual = keep.tile([P, CHUNKS, N], F32, name="residual")
        xa_plane = [[keep.tile([P, T], F32, name="xa_%d_%d" % (z, t)) for t in range(PACK)] for z in range(PASSES)]
        xb_pair = [[keep.tile([P, 2 * S], F32, name="xb_%d_%d" % (z, h)) for h in range(2)] for z in range(PASSES)]

        nc.vector.memset(w_scale_raw[:].bitcast(I32), 0)
        nc.vector.memset(wb_scale[:].bitcast(I32), 0)

        warm_in = keep.tile([P, 1], F32, name="warm_in")
        warm_out = keep.tile([P, 1], F32, name="warm_out")
        nc.vector.memset(warm_in[:], 0.0)
        nc.scalar.activation(warm_out[:], warm_in[:], ACT.Copy)

        def load_w_scales():
            for q in range(QUADRANTS):
                nc.sync.dma_start(
                    out=w_scale_raw[32 * q : 32 * q + 4, :, :].bitcast(I32),
                    in_=w_scales[:, 4 * q : 4 * q + 4, :].rearrange("z r c -> r z c").bitcast(I32),
                )

        def load_wb_scales():
            for q in range(QUADRANTS):
                nc.sync.dma_start(
                    out=wb_scale[32 * q : 32 * q + 4, :].bitcast(I32),
                    in_=wb_scales[0, 4 * q : 4 * q + 4, :].bitcast(I32),
                )

        def load_xb(z, h):
            rows = xb[z * K_PASS : (z + 1) * K_PASS, :].rearrange("(p t) s -> p (t s)", t=PACK)
            nc.sync.dma_start(out=xb_pair[z][h][:], in_=rows[:, 2 * h * S : (2 * h + 2) * S])

        def load_xa(z, t):
            rows = xa[z * K_PASS : (z + 1) * K_PASS, :].rearrange("(p t) c -> p (t c)", t=PACK)
            nc.sync.dma_start(out=xa_plane[z][t][:], in_=rows[:, t * T : (t + 1) * T])

        load_xb(0, 0)
        nc.sync.dma_start(list_b[:], offs2)
        load_xa(0, 0)
        nc.sync.dma_start(list_a[:], offs)
        nc.sync.dma_start(out=factor[:], in_=fk.rearrange("(z p t) o -> p z (t o)", z=PASSES, t=PACK))
        load_xa(0, 1)
        nc.sync.dma_start(out=w_raw[:].bitcast(I32), in_=w_words.rearrange("z p b -> p z b").bitcast(I32))
        load_w_scales()
        load_xb(0, 1)
        load_xa(0, 2)
        load_xa(0, 3)
        for h in range(2):
            load_xb(1, h)
        for t in range(PACK):
            load_xa(1, t)
        nc.sync.dma_start(out=wb_codes[:].bitcast(I32), in_=wb_words[0].bitcast(I32))
        load_wb_scales()
        nc.sync.dma_start(out=residual[:], in_=rs.rearrange("(c p) n -> p c n", p=P))

        nc.vector.tensor_copy(
            out=w_codes[:].rearrange("p z (t c i) -> p z c t i", t=PACK, i=8),
            in_=w_raw[:].rearrange("p z (c i t) -> p z c t i", t=PACK, i=8),
        )

        nc.vector.tensor_copy(
            out=w_scale[:].rearrange("p z (t c i) -> p z c t i", t=PACK, i=16),
            in_=w_scale_raw[:].rearrange("p z (c i t) -> p z c t i", t=PACK, i=16),
        )

        a_bank = [psum.tile([P, PACK, CHUNK], F32, name="a_%d" % c) for c in range(CHUNKS)]
        p_bank = [psum.tile([P, N], F32, name="p_%d" % c) for c in range(CHUNKS)]

        def interleave(engine_copy, grouped, planes):
            engine_copy(
                out=grouped.rearrange("p (c i t) -> p c t i", t=PACK, i=4),
                in_=planes.rearrange("p t (c i) -> p c t i", i=4),
            )

        def first_matmuls(z, c, codes, scales):
            for t in range(PACK):
                cols = slice(t * P, (t + 1) * P)
                nc.tensor.matmul_mx(
                    out=a_bank[c][:, t, :],
                    lhsT=w_codes[:, z, cols].bitcast(FP4X4),
                    lhsT_scale=w_scale[:, z, cols],
                    rhs=codes.bitcast(FP8X4),
                    rhs_scale=scales,
                    start=(z == 0 and t == 0),
                    stop=(z == PASSES - 1 and t == PACK - 1),
                )

        spans = [[(0, J)], [(c * CHUNK, CHUNK) for c in range(CHUNKS)]]
        u_planes = [
            [keep.tile([P, PACK, width], F32, name="u_planes_%d_%d" % (z, first)) for first, width in spans[z]]
            for z in range(PASSES)
        ]

        def pick_b(z, t):
            h, odd = divmod(t, 2)
            picked_b = keep.tile([P, J], F32, name="picked_b_%d_%d" % (z, t))
            if odd:
                nc.vector.tensor_copy(out=picked_b[:], in_=xb_pair[z][h][:, S : 2 * S].indirect(list_b[:]))
            else:
                nc.scalar.activation(picked_b[:], xb_pair[z][h][:].indirect(list_b[:]), ACT.Copy)
            return picked_b

        def pick_a(z, t, first, width):
            picked_a = keep.tile([P, width], F32, name="picked_a_%d_%d_%d" % (z, t, first))
            listed = xa_plane[z][t][:].indirect(list_a[:, first // 16 : (first + width) // 16])
            nc.scalar.activation(picked_a[:], listed, ACT.Copy)
            return picked_a

        def product(z, t, s, a_cols, picked_b):
            first, width = spans[z][s]
            nc.vector.scalar_tensor_tensor(
                out=u_planes[z][s][:, t, :],
                in0=a_cols,
                scalar=factor[:, z, t : t + 1],
                in1=picked_b[:, first : first + width],
                op0=ALU.mult,
                op1=ALU.mult,
            )

        def fused_product(z, t, picked_b):
            scaled_b = keep.tile([P, CHUNK], F32, name="scaled_b_%d" % t)
            nc.vector.tensor_scalar(
                out=scaled_b[:], in0=picked_b[:, :CHUNK], scalar1=factor[:, z, t : t + 1], scalar2=None, op0=ALU.mult
            )
            listed = xa_plane[z][t][:].indirect(list_a[:, :LIST_COLS])
            nc.vector.tensor_tensor(out=u_planes[z][0][:, t, :], in0=listed, in1=scaled_b[:], op=ALU.mult)

        def quantise_and_multiply(z, s, engine_copy):
            first, width = spans[z][s]
            grouped = keep.tile([P, width * PACK], BF16, name="u_grouped_%d_%d" % (z, s), align_bytes=64)
            codes = keep.tile([P, width], U32, name="u_codes_%d_%d" % (z, s), align_bytes=64)
            scales = keep.tile([P, width], U8, name="u_scale_%d_%d" % (z, s), align_bytes=64)
            interleave(engine_copy, grouped[:], u_planes[z][s][:])
            nc.vector.quantize_mx(out=codes[:].bitcast(FP8X4), scales=scales[:], in_=grouped[:])
            for col in range(0, width, CHUNK):
                first_matmuls(z, (first + col) // CHUNK, codes[:, col : col + CHUNK], scales[:, col : col + CHUNK])

        for z in range(PASSES):
            for t in range(PACK):
                picked_b = pick_b(z, t)
                late = z == PASSES - 1 and t >= PACK - LATE_PLANES
                if not late:
                    picked_a = pick_a(z, t, 0, J)
                for s, (first, width) in enumerate(spans[z]):
                    if not late:
                        product(z, t, s, picked_a[:, first : first + width], picked_b)
                    elif s == 0:
                        fused_product(z, t, picked_b)
                    else:
                        product(z, t, s, pick_a(z, t, first, width)[:], picked_b)
                    if t == PACK - 1:
                        quantise_and_multiply(z, s, nc.scalar.copy if s > 0 else nc.vector.tensor_copy)

        groups = CHUNK // BUNDLE
        means = [keep.tile([P, groups, PACK], F32, name="means_%d" % c) for c in range(CHUNKS)]
        hid = [keep.tile([P, CHUNK * PACK], BF16, name="hid_%d" % c, align_bytes=64) for c in range(CHUNKS)]
        level = [keep.tile([P, 1], F32, name="level_%d" % c) for c in range(CHUNKS)]

        def bundle_means(c):
            sums = keep.tile([P, groups, PACK], F32, name="sums_%d" % c)
            nc.vector.tensor_reduce(
                out=sums[:], in_=a_bank[c][:].rearrange("p t (g i) -> p g t i", i=BUNDLE), axis=AXIS.X, op=ALU.add
            )
            nc.scalar.activation(means[c][:], sums[:], ACT.Copy, scale=1.0 / BUNDLE)

        def take_means_off(c):
            nc.vector.tensor_tensor(
                out=hid[c][:].rearrange("p (g i t) -> p g i t", i=BUNDLE, t=PACK),
                in0=a_bank[c][:].rearrange("p t (g i) -> p g i t", i=BUNDLE),
                in1=means[c][:].unsqueeze(2).to_broadcast([P, groups, BUNDLE, PACK]),
                op=ALU.subtract,
            )

        def second_product(c):
            hid_codes = keep.tile([P, CHUNK], U32, name="hid_codes_%d" % c, align_bytes=64)
            hid_scale = keep.tile([P, CHUNK], U8, name="hid_scale_%d" % c, align_bytes=64)
            magnitude = keep.tile([P, N], F32, name="magnitude_%d" % c)
            nc.vector.quantize_mx(out=hid_codes[:].bitcast(FP8X4), scales=hid_scale[:], in_=hid[c][:])
            nc.tensor.matmul_mx(
                out=p_bank[c][:],
                lhsT=hid_codes[:].bitcast(FP8X4),
                lhsT_scale=hid_scale[:],
                rhs=wb_codes[:].bitcast(FP4X4),
                rhs_scale=wb_scale[:],
                start=True,
                stop=True,
            )
            nc.scalar.activation(magnitude[:], p_bank[c][:], ACT.Abs, scale=1.0 / N, accum_out=level[c][:])

        def finish(c):
            above = keep.tile([P, N], F32, name="above_%d" % c)
            result = keep.tile([P, N], F32, name="result_%d" % c)
            if c == 0:
                minus_level = keep.tile([P, 1], F32, name="minus_level")
                nc.scalar.activation(minus_level[:], level[c][:], ACT.Copy, scale=-1.0)
                nc.scalar.activation(above[:], p_bank[c][:], ACT.Relu, bias=minus_level[:])
            else:
                nc.vector.tensor_scalar(
                    out=above[:], in0=p_bank[c][:], scalar1=level[c][:], scalar2=0.0, op0=ALU.subtract, op1=ALU.max
                )
            nc.vector.scalar_tensor_tensor(
                out=result[:], in0=residual[:, c, :], scalar=-0.3, in1=above[:], op0=ALU.mult, op1=ALU.add
            )
            nc.sync.dma_start(out=out[c * CHUNK : (c + 1) * CHUNK, :], in_=result[:])

        bundle_means(0)
        bundle_means(1)
        take_means_off(0)
        take_means_off(1)
        bundle_means(2)
        second_product(0)
        second_product(1)
        take_means_off(2)
        second_product(2)
        for c in range(CHUNKS):
            finish(c)
